import numpy as np
import ml_dtypes


def mxq(x, axis, fmt="e4m3"):
    dtype, down = {"e4m3": (ml_dtypes.float8_e4m3fn, 7), "e5m2": (ml_dtypes.float8_e5m2, 14)}[fmt]
    v = np.moveaxis(np.asarray(x, np.float32).astype(ml_dtypes.bfloat16).astype(np.float64), axis, -1)
    blocks = v.reshape(v.shape[:-1] + (-1, 32))
    amax = np.abs(blocks).max(-1, keepdims=True)
    byte = np.maximum(np.where(amax > 0, np.frexp(amax)[1] - 1 + 127, 0) - down, 1)
    scale = np.exp2(byte - 127.0)
    codes = (blocks / scale).astype(np.float32).astype(dtype).astype(np.float64)
    return np.moveaxis((codes * scale).reshape(v.shape), -1, axis)


WIDE = False


def mx_kscale(k):
    if not WIDE:
        return np.ones(k)
    levels = np.array([10, -10, 5, -5, 0])
    if k % 512:
        return np.exp2(np.random.permutation(np.resize(levels, k // 32))).repeat(32)
    a = np.empty((k // 512, 16))
    for p in range(k // 512):
        a[p, :8] = np.random.permutation(np.resize(levels, 8))
        for g in range(8):
            far = levels[np.abs(levels - a[p, g]) >= 10]
            a[p, g + 8] = far[np.random.randint(len(far))]
    return np.exp2(a.ravel()).repeat(32)


def f64(x):
    return np.asarray(x).astype(np.float64)


def striped(idx):
    return np.tile(idx.reshape(-1, 16).T, (8, 1)).astype(np.uint16)


def unstriped(offs):
    return offs[:16].T.reshape(-1).astype(np.int64)


def striped8(idx):
    return np.concatenate([x.reshape(-1, 16).T for x in idx]).astype(np.uint16)


def runs(offs, k):
    lists = np.stack([offs[16 * r : 16 * r + 16].T.reshape(-1) for r in range(8)]).astype(np.int64)
    return lists[np.arange(k) % 512 // 64]


def pack_weight(w):
    k, n = w.shape
    w = f64(np.asarray(w, np.float32).astype(ml_dtypes.bfloat16)).reshape(k // 32, 32, n)
    amax = np.abs(w).max(1)
    byte = np.clip(np.where(amax > 0, np.frexp(amax)[1] - 1 + 127 - 7, 1), 1, 254)
    scaled = (w * np.exp2(127.0 - byte)[:, None, :]).reshape(k, n).astype(np.float32)
    words = np.ascontiguousarray(scaled.reshape(k // 512, 128, 4, n).transpose(0, 1, 3, 2)).astype(ml_dtypes.float8_e4m3fn).view(np.uint8)
    return words, np.ascontiguousarray(byte.astype(np.uint8).reshape(k // 512, 16, n))


def unpack_weight(words, scales):
    g, p, n, _ = words.shape
    vals = np.ascontiguousarray(words).view(ml_dtypes.float8_e4m3fn).astype(np.float64) * np.repeat(np.exp2(scales.astype(np.float64) - 127.0), 8, axis=1)[..., None]
    return vals.transpose(0, 1, 3, 2).reshape(g * 512, n)


K, T, S, N, G, H, W, U = 512, 2048, 512, 512, 2048, 512, 256, 1024


def setup_inputs():
    n = np.random.standard_normal
    s = mx_kscale(K)[:, None]
    u = mx_kscale(S)
    packed_xT = pack_weight(n((K, T)) * s)
    packed_dT = pack_weight(n((K, G)) / s)
    perm = np.stack([np.random.permutation(S) for _ in range(8)])
    perm2 = np.stack([np.random.permutation(U) for _ in range(8)])
    return {
        "x_words": packed_xT[0],
        "x_scales": packed_xT[1],
        "d_words": packed_dT[0],
        "d_scales": packed_dT[1],
        "gn": (np.random.uniform(0.5, 1.5, (H, 1)) * u[:, None]).astype(np.float32),
        "w1": (n((H, N)) / np.sqrt(H) / u[:, None]).astype(np.float32),
        "offs": striped(np.random.permutation(T)[:S]),
        "kidx": striped8(np.random.randint(0, G, (8, H))),
        "n1": striped8(perm[:, :W]),
        "n2": striped8(perm[:, W:]),
        "n3": striped8(perm2[:, :S]),
        "n4": striped8(perm2[:, S:]),
        "n5": striped8(np.stack([np.random.permutation(S) for _ in range(8)])),
    }


def reference(x_words, x_scales, d_words, d_scales, gn, w1, offs, kidx, n1, n2, n3, n4, n5):
    d_kidx = unpack_weight(d_words, d_scales)[np.arange(K)[:, None], runs(kidx, K)]
    xq = unpack_weight(x_words, x_scales)[:, unstriped(offs)]
    s = 0.0625 * (d_kidx.T @ xq)
    pa = s[np.arange(H)[:, None], runs(n1, H)]
    pb = s[np.arange(H)[:, None], runs(n2, H)]
    ra = np.maximum(pa, pb)
    ds = s.copy()
    ds[np.arange(H)[:, None], runs(n1, H)] = ra
    z = f64(gn) * ds
    h = mxq(f64(w1), 0, "e4m3").T @ mxq(z, 0, "e4m3")
    nw = h - (h[np.arange(N)[:, None], runs(n5, N)])
    ph = np.zeros((N, U))
    ph[np.arange(N)[:, None], runs(n3, N)] = h
    out = ph.copy()
    out[np.arange(N)[:, None], runs(n4, N)] = nw
    return out

@@ -1,0 +1,140 @@
+from contextlib import ExitStack
+
+import concourse.mybir as mybir
+
+F32 = mybir.dt.float32
+BF16 = mybir.dt.bfloat16
+I32 = mybir.dt.int32
+U32 = mybir.dt.uint32
+U16 = mybir.dt.uint16
+U8 = mybir.dt.uint8
+FP8X4 = mybir.dt.float8_e4m3fn_x4
+COPY = mybir.ActivationFunctionType.Copy
+ALU = mybir.AluOpType
+
+P = 128
+PACK = 4
+TABLE = 2048
+S = 512
+PAIRS = 256
+PAGE = 1024
+CHUNKS = ((0, 128), (128, 128), (256, 256))
+
+FLOPS = 2 * 2 * 512 * 512 * 512
+
+
+def tile_picked_keyfillpagq_none_p_kernel(tc, x_words, x_scales, d_words, d_scales, gn, w1, offs, kidx, n1, n2, n3, n4, n5, out):
+    nc = tc.nc
+    with ExitStack() as ctx:
+        keep = ctx.enter_context(tc.tile_pool(name="keep", bufs=1))
+        psum = ctx.enter_context(tc.psum_pool(name="psum", bufs=1))
+
+        def sb(name, shape, dtype):
+            return keep.tile(shape, dtype, name=name, align_bytes=64)
+
+        def load_list(name, src):
+            t = sb(name, list(src.shape), U16)
+            nc.sync.dma_start(t[:], src)
+            return t
+
+        d_tab = sb("d_tab", [P, TABLE], U32)
+        x_tab = sb("x_tab", [P, TABLE], U32)
+        d_stab = sb("d_stab", [P, TABLE], U8)
+        x_stab = sb("x_stab", [P, TABLE], U8)
+        d_splane = sb("d_splane", [P, S], U8)
+        nc.vector.memset(x_stab[:].bitcast(I32), 0)
+
+        kidx_t = load_list("kidx_t", kidx)
+        nc.scalar.dma_start(d_stab[:].bitcast(I32), d_scales[0].bitcast(I32).unsqueeze(1).to_broadcast([16, 8, TABLE // 4]))
+        offs_t = load_list("offs_t", offs)
+        n1_t = load_list("n1_t", n1)
+        n2_t = load_list("n2_t", n2)
+        n3_t = load_list("n3_t", n3)
+        nc.sync.dma_start(d_tab[:].bitcast(I32), d_words[0].rearrange("p n t -> p (n t)").bitcast(I32))
+        n5_t = load_list("n5_t", n5)
+        n4_t = load_list("n4_t", n4)
+        x_rows = x_scales[0].bitcast(I32)
+        for q in range(4):
+            nc.scalar.dma_start(x_stab[32 * q : 32 * q + 4, :].bitcast(I32), x_rows[4 * q : 4 * q + 4, :])
+        nc.sync.dma_start(x_tab[:].bitcast(I32), x_words[0].rearrange("p n t -> p (n t)").bitcast(I32))
+
+        d_sg = sb("d_sg", [P, S], U8)
+        nc.vector.tensor_copy(d_sg[:], d_stab[:].indirect(kidx_t[:]))
+        d_sdealt = keep.tile([P, S], U8, name="d_sdealt", tag="dealt_then_w", align_bytes=64)
+        nc.vector.tensor_copy(d_sdealt[:].rearrange("p (t m) -> p t m", t=PACK), d_sg[:].rearrange("p (m t) -> p t m", t=PACK))
+        nc.vector.tensor_copy(d_splane[:].bitcast(I32), d_sdealt[:].bitcast(I32))
+        for r in range(1, 4):
+            src = 8 * r
+            nc.scalar.dma_start(d_splane[r:P:32, :].bitcast(I32), d_sdealt[src:P:32, :].bitcast(I32))
+
+        w_raw = keep.tile([P, PACK, S], F32, name="w_raw", tag="dealt_then_w", align_bytes=64)
+        nc.sync.dma_start(w_raw[:], w1.rearrange("(p j) m -> p j m", j=PACK))
+        gain = sb("gain", [P, PACK], F32)
+        nc.gpsimd.dma_start(gain[:], gn.rearrange("(p t) o -> p (t o)", t=PACK))
+
+        x_sg = sb("x_sg", [P, S], U8)
+        nc.vector.tensor_copy(x_sg[:], x_stab[:].indirect(offs_t[:]))
+        d_g = sb("d_g", [P, S], U32)
+        nc.vector.tensor_copy(d_g[:], d_tab[:].indirect(kidx_t[:]))
+        d_dealt = sb("d_dealt", [P, S], U32)
+        nc.vector.tensor_copy(d_dealt[:].rearrange("p (t m) -> p t m", t=PACK), d_g[:].rearrange("p (m t) -> p t m", t=PACK))
+        x_g = sb("x_g", [P, S], U32)
+        nc.vector.tensor_copy(x_g[:], x_tab[:].indirect(offs_t[:]))
+
+        scores = []
+        for t in range(PACK):
+            cols = slice(t * P, (t + 1) * P)
+            acc = psum.tile([P, S], F32, name=f"s_acc{t}")
+            nc.tensor.matmul_mx(out=acc[:], lhsT=d_dealt[:, cols].bitcast(FP8X4), lhsT_scale=d_splane[:, cols], rhs=x_g[:].bitcast(FP8X4), rhs_scale=x_sg[:], start=True, stop=True)
+            s_t = sb(f"s{t}", [P, S], F32)
+            nc.scalar.activation(s_t[:], acc[:], COPY, scale=0.0625)
+            pa = sb(f"pa{t}", [P, PAIRS], F32)
+            pb = sb(f"pb{t}", [P, PAIRS], F32)
+            if t == 0:
+                nc.vector.tensor_copy(pa[:], s_t[:].indirect(n1_t[:]))
+            else:
+                nc.scalar.activation(pa[:], s_t[:].indirect(n1_t[:]), COPY)
+            nc.scalar.activation(pb[:], s_t[:].indirect(n2_t[:]), COPY)
+            ra = sb(f"ra{t}", [P, PAIRS], F32)
+            nc.vector.tensor_tensor(ra[:], pa[:], pb[:], ALU.max)
+            nc.vector.tensor_copy(s_t[:].indirect(n1_t[:]), ra[:])
+            scores.append(s_t)
+
+        w_grouped = sb("w_grouped", [P, S * PACK], BF16)
+        nc.scalar.copy(w_grouped[:].rearrange("p (t m j) -> p m j t", t=PACK, j=PACK), w_raw[:].rearrange("p j (m t) -> p m j t", t=PACK))
+        w_codes = sb("w_codes", [P, S], U32)
+        w_scales = sb("w_scales", [P, S], U8)
+        nc.vector.quantize_mx(out=w_codes[:].bitcast(FP8X4), scales=w_scales[:], in_=w_grouped[:])
+
+        sums = [sb(f"h{t}", [P, S], F32) for t in range(PACK)]
+        pages = [sb(f"page{t}", [P, PAGE], F32) for t in range(PACK)]
+        for c, (j0, n) in enumerate(CHUNKS):
+            z = sb(f"z{c}", [P, n, PACK], BF16)
+            for t in range(PACK):
+                if c == 0 and t >= 2:
+                    nc.vector.tensor_scalar(z[:, :, t], scores[t][:, j0 : j0 + n], gain[:, t : t + 1], None, ALU.mult)
+                else:
+                    nc.scalar.activation(z[:, :, t], scores[t][:, j0 : j0 + n], COPY, scale=gain[:, t : t + 1])
+            z_codes = sb(f"z_codes{c}", [P, n], U32)
+            z_scales = sb(f"z_scales{c}", [P, n], U8)
+            nc.vector.quantize_mx(out=z_codes[:].bitcast(FP8X4), scales=z_scales[:], in_=z[:].rearrange("p n t -> p (n t)"))
+            per_bank = 512 // n
+            for b in range(PACK // per_bank):
+                acc = psum.tile([P, per_bank, n], F32, name=f"h_acc{c}_{b}")
+                for u in range(per_bank):
+                    cols = slice((b * per_bank + u) * P, (b * per_bank + u + 1) * P)
+                    nc.tensor.matmul_mx(out=acc[:, u, :], lhsT=w_codes[:, cols].bitcast(FP8X4), lhsT_scale=w_scales[:, cols], rhs=z_codes[:].bitcast(FP8X4), rhs_scale=z_scales[:], start=True, stop=True)
+                for u in range(per_bank):
+                    t = b * per_bank + u
+                    nc.scalar.copy(sums[t][:, j0 : j0 + n], acc[:, u, :])
+            for t in range(PACK):
+                if True:
+                    nc.vector.tensor_copy(pages[t][:].indirect(n3_t[:, j0 // 16 : (j0 + n) // 16]), sums[t][:, j0 : j0 + n])
+
+        out_rows = out.rearrange("(p t) w -> t p w", t=PACK)
+        for t in range(PACK):
+            minus = sb(f"minus{t}", [P, S], F32)
+            for j0 in range(0, S, PAIRS):
+                nc.scalar.activation(minus[:, j0 : j0 + PAIRS], sums[t][:].indirect(n5_t[:, j0 // 16 : (j0 + PAIRS) // 16]), COPY, scale=-1.0)
+            nc.vector.tensor_tensor(pages[t][:].indirect(n4_t[:]), sums[t][:], minus[:], ALU.add)
+            nc.sync.dma_start(out_rows[t], pages[t][:])

@@ -18,7 +18,10 @@ TABLE = 2048
 S = 512
 PAIRS = 256
 PAGE = 1024
-CHUNKS = ((0, 128), (128, 128), (256, 256))
+HALF = S // 2
+RUN = 8
+SCORE_SCALE = 0.0625
+FIRST = 256
 
 FLOPS = 2 * 2 * 512 * 512 * 512
 
@@ -42,52 +45,71 @@ def tile_picked_keyfillpagq_none_p_kernel(tc, x_words, x_scales, d_words, d_scal
         d_stab = sb("d_stab", [P, TABLE], U8)
         x_stab = sb("x_stab", [P, TABLE], U8)
         d_splane = sb("d_splane", [P, S], U8)
+        nc.vector.memset(d_stab[:].bitcast(I32), 0)
         nc.vector.memset(x_stab[:].bitcast(I32), 0)
 
         kidx_t = load_list("kidx_t", kidx)
-        nc.scalar.dma_start(d_stab[:].bitcast(I32), d_scales[0].bitcast(I32).unsqueeze(1).to_broadcast([16, 8, TABLE // 4]))
-        offs_t = load_list("offs_t", offs)
-        n1_t = load_list("n1_t", n1)
-        n2_t = load_list("n2_t", n2)
-        n3_t = load_list("n3_t", n3)
+        d_rows = d_scales[0].bitcast(I32).rearrange("(g r) n -> r g n", r=2)
+        for r in range(2):
+            nc.scalar.dma_start(d_stab[r:P:16, :].bitcast(I32), d_rows[r])
         nc.sync.dma_start(d_tab[:].bitcast(I32), d_words[0].rearrange("p n t -> p (n t)").bitcast(I32))
-        n5_t = load_list("n5_t", n5)
-        n4_t = load_list("n4_t", n4)
+        offs_t = load_list("offs_t", offs)
+        nc.sync.dma_start(x_tab[:].bitcast(I32), x_words[0].rearrange("p n t -> p (n t)").bitcast(I32))
         x_rows = x_scales[0].bitcast(I32)
         for q in range(4):
             nc.scalar.dma_start(x_stab[32 * q : 32 * q + 4, :].bitcast(I32), x_rows[4 * q : 4 * q + 4, :])
-        nc.sync.dma_start(x_tab[:].bitcast(I32), x_words[0].rearrange("p n t -> p (n t)").bitcast(I32))
-
-        d_sg = sb("d_sg", [P, S], U8)
-        nc.vector.tensor_copy(d_sg[:], d_stab[:].indirect(kidx_t[:]))
-        d_sdealt = keep.tile([P, S], U8, name="d_sdealt", tag="dealt_then_w", align_bytes=64)
-        nc.vector.tensor_copy(d_sdealt[:].rearrange("p (t m) -> p t m", t=PACK), d_sg[:].rearrange("p (m t) -> p t m", t=PACK))
-        nc.vector.tensor_copy(d_splane[:].bitcast(I32), d_sdealt[:].bitcast(I32))
-        for r in range(1, 4):
-            src = 8 * r
-            nc.scalar.dma_start(d_splane[r:P:32, :].bitcast(I32), d_sdealt[src:P:32, :].bitcast(I32))
-
-        w_raw = keep.tile([P, PACK, S], F32, name="w_raw", tag="dealt_then_w", align_bytes=64)
+        n1_t = load_list("n1_t", n1)
+        n2_t = load_list("n2_t", n2)
+        n3_t = load_list("n3_t", n3)
+        n5_t = load_list("n5_t", n5)
+        n4_t = load_list("n4_t", n4)
+        w_raw = sb("w_raw", [P, PACK, S], F32)
         nc.sync.dma_start(w_raw[:], w1.rearrange("(p j) m -> p j m", j=PACK))
         gain = sb("gain", [P, PACK], F32)
         nc.gpsimd.dma_start(gain[:], gn.rearrange("(p t) o -> p (t o)", t=PACK))
 
-        x_sg = sb("x_sg", [P, S], U8)
-        nc.vector.tensor_copy(x_sg[:], x_stab[:].indirect(offs_t[:]))
+        d_sg = sb("d_sg", [P, S], U8)
+        nc.vector.tensor_copy(d_sg[:], d_stab[:].indirect(kidx_t[:]))
+        d_sdealt = sb("d_sdealt", [P, S], U8)
+        nc.vector.tensor_copy(d_sdealt[:].rearrange("p (t m) -> p m t", t=PACK), d_sg[:].rearrange("p (m t) -> p m t", t=PACK))
+        nc.vector.tensor_copy(d_splane[:].bitcast(I32), d_sdealt[:].bitcast(I32))
+        for r in range(2):
+            nc.scalar.dma_start(d_splane[2 + r : P : 32, :].bitcast(I32), d_sdealt[16 + r : P : 32, :].bitcast(I32))
+
         d_g = sb("d_g", [P, S], U32)
         nc.vector.tensor_copy(d_g[:], d_tab[:].indirect(kidx_t[:]))
         d_dealt = sb("d_dealt", [P, S], U32)
-        nc.vector.tensor_copy(d_dealt[:].rearrange("p (t m) -> p t m", t=PACK), d_g[:].rearrange("p (m t) -> p t m", t=PACK))
-        x_g = sb("x_g", [P, S], U32)
-        nc.vector.tensor_copy(x_g[:], x_tab[:].indirect(offs_t[:]))
+        nc.vector.tensor_copy(d_dealt[:].rearrange("p (t m) -> p m t", t=PACK), d_g[:].rearrange("p (m t) -> p m t", t=PACK))
+        x_sg = sb("x_sg", [P, S], U8)
+        nc.vector.tensor_copy(x_sg[:], x_stab[:].indirect(offs_t[:]))
+        x_g = [sb(f"x_g{c}", [P, HALF], U32) for c in range(2)]
+        for c in range(2):
+            nc.vector.tensor_copy(x_g[c][:], x_tab[:].indirect(offs_t[:, c * HALF // 16 : (c + 1) * HALF // 16]))
 
+        def bank(i, name):
+            return psum.tile([P, S], F32, name=name, tag=f"bank{i}")
+
+        def mx(acc, lhs_codes, lhs_scales, rhs_codes, rhs_scales):
+            nc.tensor.matmul_mx(out=acc, lhsT=lhs_codes.bitcast(FP8X4), lhsT_scale=lhs_scales, rhs=rhs_codes.bitcast(FP8X4), rhs_scale=rhs_scales, start=True, stop=True)
+
+        halves = [slice(c * HALF, (c + 1) * HALF) for c in range(2)]
         scores = []
         for t in range(PACK):
             cols = slice(t * P, (t + 1) * P)
-            acc = psum.tile([P, S], F32, name=f"s_acc{t}")
-            nc.tensor.matmul_mx(out=acc[:], lhsT=d_dealt[:, cols].bitcast(FP8X4), lhsT_scale=d_splane[:, cols], rhs=x_g[:].bitcast(FP8X4), rhs_scale=x_sg[:], start=True, stop=True)
             s_t = sb(f"s{t}", [P, S], F32)
-            nc.scalar.activation(s_t[:], acc[:], COPY, scale=0.0625)
+            if t == 0:
+                for c in range(2):
+                    acc = bank(c, f"s_acc0_{c}")
+                    mx(acc[:, :HALF], d_dealt[:, cols], d_splane[:, cols], x_g[c][:], x_sg[:, halves[c]])
+                    if c == 0:
+                        nc.scalar.activation(s_t[:, halves[c]], acc[:, :HALF], COPY, scale=SCORE_SCALE)
+                    else:
+                        nc.vector.tensor_scalar(s_t[:, halves[c]], acc[:, :HALF], SCORE_SCALE, None, ALU.mult)
+            else:
+                acc = bank(t + 1, f"s_acc{t}")
+                for c in range(2):
+                    mx(acc[:, halves[c]], d_dealt[:, cols], d_splane[:, cols], x_g[c][:], x_sg[:, halves[c]])
+                nc.scalar.activation(s_t[:], acc[:], COPY, scale=SCORE_SCALE)
             pa = sb(f"pa{t}", [P, PAIRS], F32)
             pb = sb(f"pb{t}", [P, PAIRS], F32)
             if t == 0:
@@ -100,41 +122,74 @@ def tile_picked_keyfillpagq_none_p_kernel(tc, x_words, x_scales, d_words, d_scal
             nc.vector.tensor_copy(s_t[:].indirect(n1_t[:]), ra[:])
             scores.append(s_t)
 
-        w_grouped = sb("w_grouped", [P, S * PACK], BF16)
-        nc.scalar.copy(w_grouped[:].rearrange("p (t m j) -> p m j t", t=PACK, j=PACK), w_raw[:].rearrange("p j (m t) -> p m j t", t=PACK))
-        w_codes = sb("w_codes", [P, S], U32)
-        w_scales = sb("w_scales", [P, S], U8)
-        nc.vector.quantize_mx(out=w_codes[:].bitcast(FP8X4), scales=w_scales[:], in_=w_grouped[:])
+        w_cols = w_raw[:].rearrange("p j (b t u) -> p t b j u", t=PACK, u=RUN)
+        w_first = sb("w_first", [P, P * PACK], BF16)
+        w_rest = sb("w_rest", [P, 3 * P * PACK], BF16)
+        nc.scalar.copy(w_first[:].rearrange("p (b u j) -> p b j u", u=RUN, j=PACK), w_cols[:, 0])
+        wf_codes = sb("wf_codes", [P, P], U32)
+        wf_scales = sb("wf_scales", [P, P], U8)
+        nc.vector.quantize_mx(out=wf_codes[:].bitcast(FP8X4), scales=wf_scales[:], in_=w_first[:])
 
         sums = [sb(f"h{t}", [P, S], F32) for t in range(PACK)]
-        pages = [sb(f"page{t}", [P, PAGE], F32) for t in range(PACK)]
-        for c, (j0, n) in enumerate(CHUNKS):
-            z = sb(f"z{c}", [P, n, PACK], BF16)
+        parts = [slice(0, FIRST), slice(FIRST, S)]
+
+        def quantise_z(c):
+            n = parts[c].stop - parts[c].start
+            planes = sb(f"z_planes{c}", [P, PACK, n], BF16)
             for t in range(PACK):
-                if c == 0 and t >= 2:
-                    nc.vector.tensor_scalar(z[:, :, t], scores[t][:, j0 : j0 + n], gain[:, t : t + 1], None, ALU.mult)
+                if c == 0 and t == PACK - 1:
+                    nc.vector.tensor_scalar(planes[:, t, :], scores[t][:, parts[c]], gain[:, t : t + 1], None, ALU.mult)
                 else:
-                    nc.scalar.activation(z[:, :, t], scores[t][:, j0 : j0 + n], COPY, scale=gain[:, t : t + 1])
+                    nc.scalar.activation(planes[:, t, :], scores[t][:, parts[c]], COPY, scale=gain[:, t : t + 1])
+            z = keep.tile([P, n, PACK], BF16, name=f"z{c}", tag=f"z{c}", align_bytes=64)
+            woven = z[:].rearrange("p (n i) t -> p n t i", i=4)
+            plain = planes[:].rearrange("p t (n i) -> p n t i", i=4)
+            if c == 0:
+                nc.vector.tensor_copy(woven, plain)
+            else:
+                nc.scalar.copy(woven, plain)
             z_codes = sb(f"z_codes{c}", [P, n], U32)
             z_scales = sb(f"z_scales{c}", [P, n], U8)
             nc.vector.quantize_mx(out=z_codes[:].bitcast(FP8X4), scales=z_scales[:], in_=z[:].rearrange("p n t -> p (n t)"))
-            per_bank = 512 // n
-            for b in range(PACK // per_bank):
-                acc = psum.tile([P, per_bank, n], F32, name=f"h_acc{c}_{b}")
-                for u in range(per_bank):
-                    cols = slice((b * per_bank + u) * P, (b * per_bank + u + 1) * P)
-                    nc.tensor.matmul_mx(out=acc[:, u, :], lhsT=w_codes[:, cols].bitcast(FP8X4), lhsT_scale=w_scales[:, cols], rhs=z_codes[:].bitcast(FP8X4), rhs_scale=z_scales[:], start=True, stop=True)
-                for u in range(per_bank):
-                    t = b * per_bank + u
-                    nc.scalar.copy(sums[t][:, j0 : j0 + n], acc[:, u, :])
-            for t in range(PACK):
-                if True:
-                    nc.vector.tensor_copy(pages[t][:].indirect(n3_t[:, j0 // 16 : (j0 + n) // 16]), sums[t][:, j0 : j0 + n])
+            return z_codes, z_scales
 
-        out_rows = out.rearrange("(p t) w -> t p w", t=PACK)
+        def product(c, t, z_codes, z_scales):
+            n = parts[c].stop - parts[c].start
+            acc = bank((5 + PACK * c + t) % 8, f"h_acc{c}_{t}")
+            for j0 in range(0, n, HALF):
+                js = slice(j0, min(j0 + HALF, n))
+                mx(acc[:, js], w_parts[t][0], w_parts[t][1], z_codes[:, js], z_scales[:, js])
+            if c == 0 and t == 0:
+                nc.vector.tensor_copy(sums[t][:, parts[c]], acc[:, :n])
+            else:
+                nc.scalar.copy(sums[t][:, parts[c]], acc[:, :n])
+
+        def put_sums(c, t):
+            nc.vector.tensor_copy(pages[t][:].indirect(n3_t[:, parts[c].start // 16 : parts[c].stop // 16]), sums[t][:, parts[c]])
+
+        z_first = quantise_z(0)
+        for t in range(1, PACK):
+            nc.scalar.copy(w_rest[:, (t - 1) * P * PACK : t * P * PACK].rearrange("p (b u j) -> p b j u", u=RUN, j=PACK), w_cols[:, t])
+        wr_codes = keep.tile([P, 3 * P], U32, name="wr_codes", tag="z0", align_bytes=64)
+        wr_scales = sb("wr_scales", [P, 3 * P], U8)
+        nc.vector.quantize_mx(out=wr_codes[:].bitcast(FP8X4), scales=wr_scales[:], in_=w_rest[:])
+        w_parts = [(wf_codes[:], wf_scales[:])] + [(wr_codes[:, i * P : (i + 1) * P], wr_scales[:, i * P : (i + 1) * P]) for i in range(3)]
+        pages = [sb(f"page{t}", [P, PAGE], F32) for t in range(PACK - 1)]
+        for t in range(PACK):
+            product(0, t, *z_first)
+        for t in range(PACK - 1):
+            put_sums(0, t)
+        z_rest = quantise_z(1)
+        pages.append(keep.tile([P, PAGE], F32, name="page3", tag="z1", align_bytes=64))
+        put_sums(0, PACK - 1)
+        for t in range(PACK):
+            product(1, t, *z_rest)
+            put_sums(1, t)
+
+        out_rows = out.rearrange("(b t u) w -> t b (u w)", t=PACK, u=RUN)
         for t in range(PACK):
             minus = sb(f"minus{t}", [P, S], F32)
-            for j0 in range(0, S, PAIRS):
-                nc.scalar.activation(minus[:, j0 : j0 + PAIRS], sums[t][:].indirect(n5_t[:, j0 // 16 : (j0 + PAIRS) // 16]), COPY, scale=-1.0)
+            for c in range(2):
+                nc.scalar.activation(minus[:, halves[c]], sums[t][:].indirect(n5_t[:, c * HALF // 16 : (c + 1) * HALF // 16]), COPY, scale=-1.0)
             nc.vector.tensor_tensor(pages[t][:].indirect(n4_t[:]), sums[t][:], minus[:], ALU.add)
             nc.sync.dma_start(out_rows[t], pages[t][:])

@@ -44,20 +44,16 @@ def tile_picked_keyfillpagq_none_p_kernel(tc, x_words, x_scales, d_words, d_scal
         x_tab = sb("x_tab", [P, TABLE], U32)
         d_stab = sb("d_stab", [P, TABLE], U8)
         x_stab = sb("x_stab", [P, TABLE], U8)
-        d_splane = sb("d_splane", [P, S], U8)
-        nc.vector.memset(d_stab[:].bitcast(I32), 0)
         nc.vector.memset(x_stab[:].bitcast(I32), 0)
 
         kidx_t = load_list("kidx_t", kidx)
-        d_rows = d_scales[0].bitcast(I32).rearrange("(g r) n -> r g n", r=2)
-        for r in range(2):
-            nc.scalar.dma_start(d_stab[r:P:16, :].bitcast(I32), d_rows[r])
-        nc.sync.dma_start(d_tab[:].bitcast(I32), d_words[0].rearrange("p n t -> p (n t)").bitcast(I32))
+        nc.scalar.dma_start(d_stab[:].bitcast(I32), d_scales[0].bitcast(I32).unsqueeze(1).to_broadcast([16, 8, TABLE // 4]))
+        nc.scalar.dma_start(d_tab[:].bitcast(I32), d_words[0].rearrange("p n t -> p (n t)").bitcast(I32))
         offs_t = load_list("offs_t", offs)
-        nc.sync.dma_start(x_tab[:].bitcast(I32), x_words[0].rearrange("p n t -> p (n t)").bitcast(I32))
         x_rows = x_scales[0].bitcast(I32)
         for q in range(4):
-            nc.scalar.dma_start(x_stab[32 * q : 32 * q + 4, :].bitcast(I32), x_rows[4 * q : 4 * q + 4, :])
+            nc.sync.dma_start(x_stab[32 * q : 32 * q + 4, :].bitcast(I32), x_rows[4 * q : 4 * q + 4, :])
+        nc.sync.dma_start(x_tab[:].bitcast(I32), x_words[0].rearrange("p n t -> p (n t)").bitcast(I32))
         n1_t = load_list("n1_t", n1)
         n2_t = load_list("n2_t", n2)
         n3_t = load_list("n3_t", n3)
@@ -70,11 +66,10 @@ def tile_picked_keyfillpagq_none_p_kernel(tc, x_words, x_scales, d_words, d_scal
 
         d_sg = sb("d_sg", [P, S], U8)
         nc.vector.tensor_copy(d_sg[:], d_stab[:].indirect(kidx_t[:]))
-        d_sdealt = sb("d_sdealt", [P, S], U8)
-        nc.vector.tensor_copy(d_sdealt[:].rearrange("p (t m) -> p m t", t=PACK), d_sg[:].rearrange("p (m t) -> p m t", t=PACK))
-        nc.vector.tensor_copy(d_splane[:].bitcast(I32), d_sdealt[:].bitcast(I32))
-        for r in range(2):
-            nc.scalar.dma_start(d_splane[2 + r : P : 32, :].bitcast(I32), d_sdealt[16 + r : P : 32, :].bitcast(I32))
+        d_splane = sb("d_splane", [P, S], U8)
+        nc.vector.tensor_copy(d_splane[:].rearrange("p (t m) -> p m t", t=PACK), d_sg[:].rearrange("p (m t) -> p m t", t=PACK))
+        for r in range(1, 4):
+            nc.scalar.dma_start(d_splane[r:P:32, :].bitcast(I32), d_splane[8 * r : P : 32, :].bitcast(I32))
 
         d_g = sb("d_g", [P, S], U32)
         nc.vector.tensor_copy(d_g[:], d_tab[:].indirect(kidx_t[:]))

@@ -67,14 +67,14 @@ def tile_picked_keyfillpagq_none_p_kernel(tc, x_words, x_scales, d_words, d_scal
         d_sg = sb("d_sg", [P, S], U8)
         nc.vector.tensor_copy(d_sg[:], d_stab[:].indirect(kidx_t[:]))
         d_splane = sb("d_splane", [P, S], U8)
-        nc.vector.tensor_copy(d_splane[:].rearrange("p (t m) -> p m t", t=PACK), d_sg[:].rearrange("p (m t) -> p m t", t=PACK))
+        nc.vector.tensor_copy(d_splane[:].rearrange("p (t a i) -> p a t i", t=PACK, i=16), d_sg[:].rearrange("p (a i t) -> p a t i", t=PACK, i=16))
         for r in range(1, 4):
             nc.scalar.dma_start(d_splane[r:P:32, :].bitcast(I32), d_splane[8 * r : P : 32, :].bitcast(I32))
 
         d_g = sb("d_g", [P, S], U32)
         nc.vector.tensor_copy(d_g[:], d_tab[:].indirect(kidx_t[:]))
         d_dealt = sb("d_dealt", [P, S], U32)
-        nc.vector.tensor_copy(d_dealt[:].rearrange("p (t m) -> p m t", t=PACK), d_g[:].rearrange("p (m t) -> p m t", t=PACK))
+        nc.vector.tensor_copy(d_dealt[:].rearrange("p (t a i) -> p a t i", t=PACK, i=4), d_g[:].rearrange("p (a i t) -> p a t i", t=PACK, i=4))
         x_sg = sb("x_sg", [P, S], U8)
         nc.vector.tensor_copy(x_sg[:], x_stab[:].indirect(offs_t[:]))
         x_g = [sb(f"x_g{c}", [P, HALF], U32) for c in range(2)]
@@ -117,10 +117,10 @@ def tile_picked_keyfillpagq_none_p_kernel(tc, x_words, x_scales, d_words, d_scal
             nc.vector.tensor_copy(s_t[:].indirect(n1_t[:]), ra[:])
             scores.append(s_t)
 
-        w_cols = w_raw[:].rearrange("p j (b t u) -> p t b j u", t=PACK, u=RUN)
+        w_cols = w_raw[:].rearrange("p j (b t a i) -> p t b a j i", t=PACK, a=2, i=4)
         w_first = sb("w_first", [P, P * PACK], BF16)
         w_rest = sb("w_rest", [P, 3 * P * PACK], BF16)
-        nc.scalar.copy(w_first[:].rearrange("p (b u j) -> p b j u", u=RUN, j=PACK), w_cols[:, 0])
+        nc.scalar.copy(w_first[:].rearrange("p (b a i j) -> p b a j i", a=2, i=4, j=PACK), w_cols[:, 0])
         wf_codes = sb("wf_codes", [P, P], U32)
         wf_scales = sb("wf_scales", [P, P], U8)
         nc.vector.quantize_mx(out=wf_codes[:].bitcast(FP8X4), scales=wf_scales[:], in_=w_first[:])
@@ -164,7 +164,7 @@ def tile_picked_keyfillpagq_none_p_kernel(tc, x_words, x_scales, d_words, d_scal
 
         z_first = quantise_z(0)
         for t in range(1, PACK):
-            nc.scalar.copy(w_rest[:, (t - 1) * P * PACK : t * P * PACK].rearrange("p (b u j) -> p b j u", u=RUN, j=PACK), w_cols[:, t])
+            nc.scalar.copy(w_rest[:, (t - 1) * P * PACK : t * P * PACK].rearrange("p (b a i j) -> p b a j i", a=2, i=4, j=PACK), w_cols[:, t])
         wr_codes = keep.tile([P, 3 * P], U32, name="wr_codes", tag="z0", align_bytes=64)
         wr_scales = sb("wr_scales", [P, 3 * P], U8)
         nc.vector.quantize_mx(out=wr_codes[:].bitcast(FP8X4), scales=wr_scales[:], in_=w_rest[:])

from contextlib import ExitStack

import concourse.mybir as mybir

F32 = mybir.dt.float32
BF16 = mybir.dt.bfloat16
I32 = mybir.dt.int32
U32 = mybir.dt.uint32
U16 = mybir.dt.uint16
U8 = mybir.dt.uint8
FP8X4 = mybir.dt.float8_e4m3fn_x4
COPY = mybir.ActivationFunctionType.Copy
ALU = mybir.AluOpType

P = 128
PACK = 4
TABLE = 2048
S = 512
PAIRS = 256
PAGE = 1024
HALF = S // 2
RUN = 8
SCORE_SCALE = 0.0625
FIRST = 256

FLOPS = 2 * 2 * 512 * 512 * 512


def tile_picked_keyfillpagq_none_p_kernel(tc, x_words, x_scales, d_words, d_scales, gn, w1, offs, kidx, n1, n2, n3, n4, n5, out):
    nc = tc.nc
    with ExitStack() as ctx:
        keep = ctx.enter_context(tc.tile_pool(name="keep", bufs=1))
        psum = ctx.enter_context(tc.psum_pool(name="psum", bufs=1))

        def sb(name, shape, dtype):
            return keep.tile(shape, dtype, name=name, align_bytes=64)

        def load_list(name, src):
            t = sb(name, list(src.shape), U16)
            nc.sync.dma_start(t[:], src)
            return t

        d_tab = sb("d_tab", [P, TABLE], U32)
        x_tab = sb("x_tab", [P, TABLE], U32)
        d_stab = sb("d_stab", [P, TABLE], U8)
        x_stab = sb("x_stab", [P, TABLE], U8)
        nc.vector.memset(x_stab[:].bitcast(I32), 0)

        kidx_t = load_list("kidx_t", kidx)
        nc.scalar.dma_start(d_stab[:].bitcast(I32), d_scales[0].bitcast(I32).unsqueeze(1).to_broadcast([16, 8, TABLE // 4]))
        nc.scalar.dma_start(d_tab[:].bitcast(I32), d_words[0].rearrange("p n t -> p (n t)").bitcast(I32))
        offs_t = load_list("offs_t", offs)
        x_rows = x_scales[0].bitcast(I32)
        for q in range(4):
            nc.sync.dma_start(x_stab[32 * q : 32 * q + 4, :].bitcast(I32), x_rows[4 * q : 4 * q + 4, :])
        nc.sync.dma_start(x_tab[:].bitcast(I32), x_words[0].rearrange("p n t -> p (n t)").bitcast(I32))
        n1_t = load_list("n1_t", n1)
        n2_t = load_list("n2_t", n2)
        n3_t = load_list("n3_t", n3)
        n5_t = load_list("n5_t", n5)
        n4_t = load_list("n4_t", n4)
        w_raw = sb("w_raw", [P, PACK, S], F32)
        nc.sync.dma_start(w_raw[:], w1.rearrange("(p j) m -> p j m", j=PACK))
        gain = sb("gain", [P, PACK], F32)
        nc.gpsimd.dma_start(gain[:], gn.rearrange("(p t) o -> p (t o)", t=PACK))

        d_sg = sb("d_sg", [P, S], U8)
        nc.vector.tensor_copy(d_sg[:], d_stab[:].indirect(kidx_t[:]))
        d_splane = sb("d_splane", [P, S], U8)
        nc.vector.tensor_copy(d_splane[:].rearrange("p (t a i) -> p a t i", t=PACK, i=16), d_sg[:].rearrange("p (a i t) -> p a t i", t=PACK, i=16))
        for r in range(1, 4):
            nc.scalar.dma_start(d_splane[r:P:32, :].bitcast(I32), d_splane[8 * r : P : 32, :].bitcast(I32))

        d_g = sb("d_g", [P, S], U32)
        nc.vector.tensor_copy(d_g[:], d_tab[:].indirect(kidx_t[:]))
        d_dealt = sb("d_dealt", [P, S], U32)
        nc.vector.tensor_copy(d_dealt[:].rearrange("p (t a i) -> p a t i", t=PACK, i=4), d_g[:].rearrange("p (a i t) -> p a t i", t=PACK, i=4))
        x_sg = sb("x_sg", [P, S], U8)
        nc.vector.tensor_copy(x_sg[:], x_stab[:].indirect(offs_t[:]))
        x_g = [sb(f"x_g{c}", [P, HALF], U32) for c in range(2)]
        for c in range(2):
            nc.vector.tensor_copy(x_g[c][:], x_tab[:].indirect(offs_t[:, c * HALF // 16 : (c + 1) * HALF // 16]))

        def bank(i, name):
            return psum.tile([P, S], F32, name=name, tag=f"bank{i}")

        def mx(acc, lhs_codes, lhs_scales, rhs_codes, rhs_scales):
            nc.tensor.matmul_mx(out=acc, lhsT=lhs_codes.bitcast(FP8X4), lhsT_scale=lhs_scales, rhs=rhs_codes.bitcast(FP8X4), rhs_scale=rhs_scales, start=True, stop=True)

        halves = [slice(c * HALF, (c + 1) * HALF) for c in range(2)]
        scores = []
        for t in range(PACK):
            cols = slice(t * P, (t + 1) * P)
            s_t = sb(f"s{t}", [P, S], F32)
            if t == 0:
                for c in range(2):
                    acc = bank(c, f"s_acc0_{c}")
                    mx(acc[:, :HALF], d_dealt[:, cols], d_splane[:, cols], x_g[c][:], x_sg[:, halves[c]])
                    if c == 0:
                        nc.scalar.activation(s_t[:, halves[c]], acc[:, :HALF], COPY, scale=SCORE_SCALE)
                    else:
                        nc.vector.tensor_scalar(s_t[:, halves[c]], acc[:, :HALF], SCORE_SCALE, None, ALU.mult)
            else:
                acc = bank(t + 1, f"s_acc{t}")
                for c in range(2):
                    mx(acc[:, halves[c]], d_dealt[:, cols], d_splane[:, cols], x_g[c][:], x_sg[:, halves[c]])
                nc.scalar.activation(s_t[:], acc[:], COPY, scale=SCORE_SCALE)
            pa = sb(f"pa{t}", [P, PAIRS], F32)
            pb = sb(f"pb{t}", [P, PAIRS], F32)
            if t == 0:
                nc.vector.tensor_copy(pa[:], s_t[:].indirect(n1_t[:]))
            else:
                nc.scalar.activation(pa[:], s_t[:].indirect(n1_t[:]), COPY)
            nc.scalar.activation(pb[:], s_t[:].indirect(n2_t[:]), COPY)
            ra = sb(f"ra{t}", [P, PAIRS], F32)
            nc.vector.tensor_tensor(ra[:], pa[:], pb[:], ALU.max)
            nc.vector.tensor_copy(s_t[:].indirect(n1_t[:]), ra[:])
            scores.append(s_t)

        w_cols = w_raw[:].rearrange("p j (b t a i) -> p t b a j i", t=PACK, a=2, i=4)
        w_first = sb("w_first", [P, P * PACK], BF16)
        w_rest = sb("w_rest", [P, 3 * P * PACK], BF16)
        nc.scalar.copy(w_first[:].rearrange("p (b a i j) -> p b a j i", a=2, i=4, j=PACK), w_cols[:, 0])
        wf_codes = sb("wf_codes", [P, P], U32)
        wf_scales = sb("wf_scales", [P, P], U8)
        nc.vector.quantize_mx(out=wf_codes[:].bitcast(FP8X4), scales=wf_scales[:], in_=w_first[:])

        sums = [sb(f"h{t}", [P, S], F32) for t in range(PACK)]
        parts = [slice(0, FIRST), slice(FIRST, S)]

        def quantise_z(c):
            n = parts[c].stop - parts[c].start
            planes = sb(f"z_planes{c}", [P, PACK, n], BF16)
            for t in range(PACK):
                if c == 0 and t == PACK - 1:
                    nc.vector.tensor_scalar(planes[:, t, :], scores[t][:, parts[c]], gain[:, t : t + 1], None, ALU.mult)
                else:
                    nc.scalar.activation(planes[:, t, :], scores[t][:, parts[c]], COPY, scale=gain[:, t : t + 1])
            z = keep.tile([P, n, PACK], BF16, name=f"z{c}", tag=f"z{c}", align_bytes=64)
            woven = z[:].rearrange("p (n i) t -> p n t i", i=4)
            plain = planes[:].rearrange("p t (n i) -> p n t i", i=4)
            if c == 0:
                nc.vector.tensor_copy(woven, plain)
            else:
                nc.scalar.copy(woven, plain)
            z_codes = sb(f"z_codes{c}", [P, n], U32)
            z_scales = sb(f"z_scales{c}", [P, n], U8)
            nc.vector.quantize_mx(out=z_codes[:].bitcast(FP8X4), scales=z_scales[:], in_=z[:].rearrange("p n t -> p (n t)"))
            return z_codes, z_scales

        def product(c, t, z_codes, z_scales):
            n = parts[c].stop - parts[c].start
            acc = bank((5 + PACK * c + t) % 8, f"h_acc{c}_{t}")
            for j0 in range(0, n, HALF):
                js = slice(j0, min(j0 + HALF, n))
                mx(acc[:, js], w_parts[t][0], w_parts[t][1], z_codes[:, js], z_scales[:, js])
            if c == 0 and t == 0:
                nc.vector.tensor_copy(sums[t][:, parts[c]], acc[:, :n])
            else:
                nc.scalar.copy(sums[t][:, parts[c]], acc[:, :n])

        def put_sums(c, t):
            nc.vector.tensor_copy(pages[t][:].indirect(n3_t[:, parts[c].start // 16 : parts[c].stop // 16]), sums[t][:, parts[c]])

        z_first = quantise_z(0)
        for t in range(1, PACK):
            nc.scalar.copy(w_rest[:, (t - 1) * P * PACK : t * P * PACK].rearrange("p (b a i j) -> p b a j i", a=2, i=4, j=PACK), w_cols[:, t])
        wr_codes = keep.tile([P, 3 * P], U32, name="wr_codes", tag="z0", align_bytes=64)
        wr_scales = sb("wr_scales", [P, 3 * P], U8)
        nc.vector.quantize_mx(out=wr_codes[:].bitcast(FP8X4), scales=wr_scales[:], in_=w_rest[:])
        w_parts = [(wf_codes[:], wf_scales[:])] + [(wr_codes[:, i * P : (i + 1) * P], wr_scales[:, i * P : (i + 1) * P]) for i in range(3)]
        pages = [sb(f"page{t}", [P, PAGE], F32) for t in range(PACK - 1)]
        for t in range(PACK):
            product(0, t, *z_first)
        for t in range(PACK - 1):
            put_sums(0, t)
        z_rest = quantise_z(1)
        pages.append(keep.tile([P, PAGE], F32, name="page3", tag="z1", align_bytes=64))
        put_sums(0, PACK - 1)
        for t in range(PACK):
            product(1, t, *z_rest)
            put_sums(1, t)

        out_rows = out.rearrange("(b t u) w -> t b (u w)", t=PACK, u=RUN)
        for t in range(PACK):
            minus = sb(f"minus{t}", [P, S], F32)
            for c in range(2):
                nc.scalar.activation(minus[:, halves[c]], sums[t][:].indirect(n5_t[:, c * HALF // 16 : (c + 1) * HALF // 16]), COPY, scale=-1.0)
            nc.vector.tensor_tensor(pages[t][:].indirect(n4_t[:]), sums[t][:], minus[:], ALU.add)
            nc.sync.dma_start(out_rows[t], pages[t][:])
